import numpy as np, ml_dtypes
CORES = [3,7,11,15,131,135,139,143]
N = 8
import mx_ref
BF = ml_dtypes.bfloat16
def gentries(a):
    return np.ascontiguousarray(a.reshape(8, 16, -1).transpose(0, 2, 1)).reshape(8, -1)
def gtable(e):
    e = np.asarray(e); return np.ascontiguousarray(e.reshape(8, -1, 16).transpose(0, 2, 1)).reshape(128, -1).astype(np.int32)
def gcols(t, e):
    v = np.concatenate([t.reshape(8, 16, -1, 4), np.zeros((8, 16, 1, 4), BF)], axis=2)
    return np.ascontiguousarray(np.stack([v[g][:, e[g]] for g in range(8)])).reshape(128, -1)
def tile(rs):
    return np.stack(rs, axis=2).reshape(128, -1).astype(BF)
def pick(q, e):
    c = np.concatenate([q[0].reshape(128, -1, 4), np.zeros((128, 1, 4), np.uint8)], axis=1); s = np.concatenate([q[1], np.ones((16, 1), np.uint8)], axis=1)
    return (np.ascontiguousarray(c[:, e].reshape(128, -1)), np.ascontiguousarray(s[:, e]))
def join(*qs):
    return (np.concatenate([q[0] for q in qs], axis=1), np.concatenate([q[1] for q in qs], axis=1))
def put(q, e, v):
    c, s = q[0].reshape(128, -1, 4).copy(), q[1].copy(); c[:, e] = v[0].reshape(128, -1, 4); s[:, e] = v[1]
    return (c.reshape(128, -1), s)
def pk(c, s):
    return (np.ascontiguousarray(c), mx_ref.live(s))
def emit(q):
    return q[0], q[1]
def packed(v, rng):
    q = [mx_ref.quantize(np.ascontiguousarray(v[r])) for r in range(N)]
    return np.stack([a for a, b in q]), np.stack([mx_ref.plane(b, rng) for a, b in q])
def values_of_codes():
    e, c = np.zeros((128, 128, 4), np.float32), np.zeros((128, 2, 4), np.uint8)
    e[np.arange(128), np.arange(128), 0] = 1
    c[:127, :, 0] = np.arange(256).reshape(2, 128).T[:127]
    return mx_ref.matmul(mx_ref.quantize(e.reshape(128, 512).astype(BF)), (c.reshape(128, 8), np.full((16, 2), 127, np.uint8))).T.reshape(-1).astype(np.float64)
CODE_VALUE, SCALE_VALUE = values_of_codes(), 2.0 ** (np.arange(256) - 127.0)
def decode(q):
    return (CODE_VALUE[q[0]].reshape(16, 8, -1, 4) * SCALE_VALUE[q[1]][:, None, :, None] + 0.0).reshape(128, -1).astype(np.float32)
def f(rng, *shape):
    return mx_ref.flush((rng.standard_normal(shape, dtype=np.float32) * np.exp2(rng.integers(-2, 3, shape[:-1] + (1,)))).astype(BF))
def wide(rng, *shape, cols=0):
    v = rng.standard_normal(shape, dtype=np.float32) * np.exp2(rng.integers(-12, 13, shape)).astype(np.float32)
    if cols: v *= np.repeat(np.exp2(rng.integers(-cols, cols + 1, shape[:-2] + (1, shape[-1] // 4))) * (rng.random(shape[:-2] + (1, shape[-1] // 4)) > 0.0625), 4, axis=-1).astype(np.float32)
    return mx_ref.flush(v.astype(BF))
C = 288
STEP = [4, 1, 2]
def numbers_of(rng):
    return {"x": np.array(f(rng, N, 128, 4 * C)), "u": np.array(f(rng, N, 128, 512)), "v": np.array(f(rng, N, 128, 512))}
def stored(w):
    return {"wl": np.stack([gtable(w[r]) for r in range(N)])}
def joined(k):
    w = np.zeros_like(k)
    np.put_along_axis(w, k[..., 0::2], k[..., 1::2], axis=-1)
    np.put_along_axis(w, k[..., 1::2], k[..., 0::2], axis=-1)
    return w
def wiring(rng):
    return stored(joined(rng.permuted(np.tile(np.arange(3 * C), (N, 8, 1)), axis=2)))
def edges(rng):
    w = np.zeros((N, 8, 3 * C), np.int64)
    c, i = np.arange(C), np.arange(3 * C)
    for r in range(N):
        a = C + rng.permutation(2 * C)
        k = [i ^ 1, 3 * C - 1 - i, (i + 3 * (C // 2)) % (3 * C), np.concatenate([c + C, c, (c ^ 1) + 2 * C]), np.concatenate([C - 1 - c, c + 2 * C, c + C]),
             joined(np.concatenate([rng.permutation(C), C + rng.permutation(2 * C)])), joined(np.concatenate([np.stack([c, a[:C]], axis=1).reshape(-1), a[C:]])), joined(rng.permutation(3 * C))]
        w[r, rng.permutation(8)] = np.stack(k)
    return stored(w)
def layers(rng):
    return np.array(f(rng, N, 128, 2048)).reshape(N, 8, 16, 4, 8, 16, 4)
def weights(rng, w):
    c, p = packed(np.ascontiguousarray(w).reshape(N, 128, 2048), rng)
    return {"wc": c, "ws": p}
def blank(d):
    u = d["u"].reshape(N, 128, 128, 4)
    u[:, :, 0::16] = 0
    u[:, :, 1::16] = 0
    return u
def setup_inputs(rng):
    return {**numbers_of(rng), **wiring(rng), **weights(rng, layers(rng))}
def setup_inputs_ties(rng):
    d = numbers_of(rng)
    o = rng.permutation(N)
    k = rng.integers(-1, 2, (N, 8, 2, C)).astype(np.float32)
    k[o[1]] = 1
    x = d["x"].reshape(N, 8, 16, C, 4)
    x[:, :, :3] = 0
    x[:, :, :2, :, 0] = k.astype(BF)
    x[:, :, 2, :, 0] = 1.96875 * 2.0 ** 7
    x[:, :, 3] = (np.array([9.0, 11.0, 5.0, 7.0]) * 2.0 ** -9).astype(np.float32).astype(BF)
    a = np.exp2(rng.integers(-3, 4, (1, 8, 1)).astype(np.float32))
    x[:, :, 8:] = 0
    x[:, :, 8, :, 0] = (-1.125 * a).astype(BF)
    x[:, :, 10, :, 0] = (-0.0703125 * a).astype(BF)
    c = np.ones(N, np.float32)
    c[o[0]] = 0
    c[o[2]] = -1
    u = blank(d)
    for h in range(0, 128, 16):
        for i in range(2): u[:, h + i, h + i, 0] = c.astype(BF)
    w = layers(rng)
    w[:, :, 2] = 0
    w[:, :, :, :, :, :4] = 0
    w[:, :, :, :, :, 8:] = 0
    for g in range(8):
        w[:, g, 8, 0, g, 8, 0] = -28.0
        for b in range(4):
            w[:, g, 10, b, g, 9, 0] = -2.0 ** (b - 5)
            w[:, g, 3, b, g, 3, b] = 64.0
    return {"x": x.reshape(N, 128, 4 * C), "u": u.reshape(N, 128, 512), "v": d["v"], **wiring(rng), **weights(rng, w)}
def setup_inputs_near(rng):
    d = numbers_of(rng)
    o = np.zeros(N, np.int64)
    for i, r in enumerate(rng.permutation([r for r in range(N) if r < (r ^ STEP[0])])):
        o[[r, r ^ STEP[0]]] = rng.permutation([0, 3] if i % 2 == 0 else [1, 2])
    x = d["x"].astype(np.float32).reshape(N, 8, 16, C, 4)
    x[:, :, :8] = 0
    u = blank(d)
    at = [0, C - 1, int(rng.integers(C)), int(rng.integers(C))]
    for r in range(N):
        s = rng.integers(-1, 2, (2, 8, C)).astype(np.float32)
        k = 2.0 ** -30 if o[r] in (0, 3) else 1.0
        for i in range(2):
            if o[r] == 2: x[r, :, 2 * i, :, 0] = s[i] * 2.0 ** -8
            else:
                x[r, :, 2 * i, :, 0] = 1.125 * k * s[i]
                x[r, :, 2 * i + 1, :, 0] = -1.25 * k * s[i]
                for g, j in zip(rng.permutation(8)[:4], at): x[r, g, 2 * i, j, 0] = 2.0 ** 30 * rng.choice([-1.0, 1.0])
            for h in range(0, 128, 16):
                u[r, h + 2 * i, h + i, 0] = 1.125 * k
                u[r, h + 2 * i + 1, h + i, 0] = k
        if o[r] == 2: x[r, :, 4, :, 0] = 1.96875 * 2.0 ** 8
        x[r, :, 5, :, 0] = rng.choice([-1.0, 1.0], (8, C)) * 2.0 ** -30
        x[r, :, 6, :, 0] = 2.0 ** -28
    w = layers(rng)
    w[:, :, :8] = 0
    w[:, :, :, :, :, :8] = 0
    for g in range(8):
        w[:, g, 5, 0, g, 0, 0] = 2.0 ** -8
        w[:, g, 5, 0, g, 2, 0] = 2.0 ** -8
        w[:, g, 5, 0, g, 6, 0] = 32.0
    return {"x": x.reshape(N, 128, 4 * C).astype(BF), "u": u.reshape(N, 128, 512), "v": d["v"], **wiring(rng), **weights(rng, w)}
def setup_inputs_late(rng):
    d = numbers_of(rng)
    c = (rng.permutation(N) % 2 * 2.0 - 1.0).astype(np.float32).astype(BF)
    x = d["x"].reshape(N, 8, 16, C, 4)
    x[:, :, :2] = c[:, None, None, None, None]
    u = blank(d)
    for h in range(0, 128, 16):
        for i in range(2): u[:, h + i, h + i, 0] = 1
    w = layers(rng)
    w[:, :, :, :, :, :2] = (w[:, :, :, :, :, :2].astype(np.float32) * 4).astype(BF)
    return {"x": x.reshape(N, 128, 4 * C), "u": u.reshape(N, 128, 512), "v": d["v"], **edges(rng), **weights(rng, w)}
def setup_inputs_ends(rng):
    d = numbers_of(rng)
    e = [0, STEP[0], STEP[1], STEP[0] ^ STEP[1]]
    e = e + [STEP[2] ^ i for i in e[:N - 4]]
    n = N // 4
    o = np.zeros(N, np.int64)
    o[np.array(e) ^ int(rng.integers(N))] = np.concatenate([np.full(n, 3), np.full(n, 2), rng.permutation(np.arange(2 * n) % 2)])
    x = np.zeros((N, 128, C, 4))
    u = blank(d).astype(np.float32)
    v = rng.choice([-1.0, 1.0], (N, 128, 512))
    w = np.zeros((N, 128, 4, 128, 4), np.float32)
    p = np.arange(128)
    for r in range(N):
        x[r] = (0.9 + 0.02 * rng.random((128, C, 4))) * 2.0 ** 30
        if o[r] == 0: x[r] *= -1
        if o[r] == 1: x[r] *= (1.0 - 2.0 * (np.arange(C) % 2))[None, :, None]
        if o[r] == 2: x[r] *= rng.choice([-1.0, 1.0], (128, C, 4))
        if o[r] == 3:
            x[r] = (1.0 + 0.125 * rng.integers(0, 8, (128, C, 4))) * 2.0 ** -30 * rng.choice([-1.0, 1.0], (1, C, 1))
            x[r, 0::8, :, 0] = 1.5 * 2.0 ** -29
        for i in range(2):
            h = rng.permutation(8)
            u[r, :, i::16] = np.where(h < 2, 0.0, h % 2 * 2.0 - 1.0)[None, :, None] * (2.0 ** -30 if o[r] == 3 else 2.0 ** 30)
        v[r] *= 2.0 ** 30 if o[r] % 2 == 0 else 2.0 ** -30
        for b in range(4): w[r, p, b, p, b] = [-0.25, -0.25, 2.0 ** -8, 256.0][o[r]]
    return {"x": x.astype(np.float32).reshape(N, 128, 4 * C).astype(BF), "u": u.reshape(N, 128, 512).astype(BF), "v": v.astype(np.float32).astype(BF), **edges(rng), **weights(rng, w.astype(BF))}
def setup_inputs_spread(rng):
    d = setup_inputs(rng)
    d["x"] = wide(rng, N, 128, 4 * C, cols=6)
    return d
def check_inputs(d):
    b = []
    for k in ("x", "u", "v"):
        a = np.abs(d[k].astype(np.float32))
        if not (np.isfinite(a).all() and ((a == 0) | (a >= 2.0 ** -30) & (a <= 2.0 ** 30)).all()): b.append("a value of " + k)
    none, least, most = [emit(mx_ref.quantize(np.full((128, 16), k, np.float32).astype(BF)))[1][0, 0] for k in (0.0, 2.0 ** -8, 2.0 ** 8)]
    for r in range(N):
        e, i = gentries(d["wl"][r]), np.arange(3 * C)
        if not ((e >= 0) & (e < 3 * C)).all(): b.append("an entry of wl")
        elif (e == i).any() or (np.take_along_axis(e, e, axis=1) != i).any(): b.append("wl: ports that aren't wired in pairs")
        if ((d["wc"][r] == 0x7F) | (d["wc"][r] == 0xFF)).any(): b.append("wc: a code that is no number")
        s = mx_ref.live(d["ws"][r])
        if ((s != none) & ((s < least) | (s > most))).any(): b.append("ws: a scale out of range")
    return b
def rewired(w, a, b):
    c, d = np.arange(C), w[:, :C]
    active = d < C
    same = a == np.take_along_axis(a, np.minimum(d, C - 1), axis=1)
    turn, cross, swap = active & same, active & ~same, ~active & b
    to = np.concatenate([np.where(turn | swap, c + C, c),
                         np.where(turn, c + 2 * C, np.where(cross, d + C, np.where(swap, c, c + C))),
                         np.where(turn, c, np.where(cross, d + 2 * C, c + 2 * C))], axis=1)
    new = np.zeros_like(to)
    np.put_along_axis(new, to, np.take_along_axis(to, w, axis=1), axis=1)
    return new
def reference(x, u, v, wl, wc, ws):
    qu = [mx_ref.quantize(u[r]) for r in range(N)]
    lay = [pk(wc[r], ws[r]) for r in range(N)]
    wire = [gentries(wl[r]).astype(np.int64) for r in range(N)]
    now = [x[r] for r in range(N)]
    for step in STEP:
        made = []
        for r in range(N):
            s = mx_ref.matmul(qu[r], mx_ref.quantize(now[r]))
            wire[r] = rewired(wire[r], s[0::16] > 0, s[1::16] > 0)
            one, two = gcols(now[r], wire[r][:, C:2 * C] % C), gcols(now[r], wire[r][:, 2 * C:] % C)
            z = mx_ref.quantize(((one.astype(np.float32) + two.astype(np.float32)) * np.float32(0.5)).astype(BF))
            made.append(mx_ref.quantize(tile([mx_ref.matmul(pick(lay[r], np.arange(128 * b, 128 * b + 128)), z) * np.float32(0.03125) for b in range(4)])))
        for r in range(N):
            p = r ^ step
            m = np.take_along_axis(wire[p], wire[r][:, :C], axis=1) % C
            now[r] = (now[r].astype(np.float32) + gcols(decode(made[p]).astype(BF), m).astype(np.float32)).astype(BF)
    y, ow = np.zeros((N, 128, C), np.float32), np.zeros((N, 8, 3 * C), np.float32)
    oc, osc = np.zeros((N, 128, 4 * C), np.uint8), np.zeros((N, 16, C), np.uint8)
    for r in range(N):
        q = mx_ref.quantize(now[r])
        y[r] = mx_ref.matmul(mx_ref.quantize(v[r]), q)
        ow[r] = wire[r]
        oc[r], osc[r] = emit(q)
    return {"y": y, "ow": ow, "oc": oc, "osc": osc}

@@ -1,0 +1,417 @@
+from concourse.mybir import dt, AluOpType as A, ActivationFunctionType as F
+
+C = 288
+STEP = [4, 1, 2]
+HUGE = 1e29
+BIG = 2097152.0
+CUT = [(0, 160), (160, 288)]
+
+_f, _b, _i, _u = "float32", "bfloat16", "int32", "uint16"
+_q, _s = "float8_e4m3fn_x4", "uint8"
+
+
+def _scratch():
+    d = {}
+
+    def sb(name, n, t):
+        d[name] = ("sbuf", [128, n], t)
+    sb("ut", 512, _b); sb("vt", 512, _b); sb("wi", 54, _i)
+    sb("wq", 512, _q); sb("wsc", 512, _s)
+    sb("uq", 128, _q); sb("us", 128, _s); sb("u2", 256, _q); sb("u2s", 256, _s)
+    sb("vq", 128, _q); sb("vs", 128, _s)
+    sb("ident", 128, _b); sb("ones", 128, _b); sb("et", 2048, _b); sb("eq", 512, _q); sb("esc", 512, _s)
+    sb("cr", C, _f); sb("cr0", C, _f); sb("t0", 2 * C, _f); sb("t1", 2 * C, _f); sb("t2", 2 * C, _f); sb("t3", 2 * C, _b)
+    sb("ei", 16, _i); sb("ea", 16, _i); sb("e0", 16, _b); sb("e1", 16, _b); sb("mf", C, _b); sb("mn", 3 * C, _b)
+    sb("bp2", 8, _f); sb("bpn", 8, _f)
+    sb("i1", 18, _i); sb("i2", 18, _i); sb("i3", 18, _i); sb("cl", 18, _f); sb("ui", 16, _i); sb("uo", 16, _u)
+    sb("pt", 1536, _f)
+    sb("c1", 54, _f); sb("c2", 54, _f); sb("c3", 54, _f)
+    for r in range(2):
+        sb("new%d" % r, 54, _i); sb("off%d" % r, 54, _u)
+    sb("al", 18, _f); sb("tl", 18, _f); sb("tm", 18, _f); sb("dp", 18, _f); sb("do", 18, _u)
+    sb("qe", 36, _f); sb("ie", 36, _f); sb("ieo", 36, _u)
+    sb("pi", 1536, _f); sb("thr", C, _b); sb("nr", 3 * C, _f); sb("ns", 3 * C, _f); sb("er", 2 * C, _f); sb("es", 2 * C, _f)
+    sb("df", 54, _f); sb("dg", 54, _f); sb("base", 54, _f); sb("dl", 54, _f); sb("bd", 54, _f); sb("base2", 54, _f)
+    sb("a2", 2 * C, _b); sb("am", C, _b); sb("fr", C, _b); sb("fs", C, _b)
+    sb("st", 54, _f); sb("sel", 54, _i); sb("xi", 54, _i); sb("xo", 54, _u)
+    sb("n0", 54, _i); sb("n1", 54, _i); sb("dn", 54, _f); sb("bb", 54, _f); sb("b2", 54, _f)
+    sb("fx", 3 * C, _b); sb("fxs", 3 * C, _b); sb("nt", 54, _f); sb("zi", 54, _i)
+    sb("zt", 1536, _f); sb("mr", C, _f); sb("ms", C, _f); sb("mo", 18, _u)
+    for r in range(4):
+        sb("x%d" % r, 4 * C, _b)
+    sb("qx", C, _q); sb("sx", C, _s); sb("qz", C, _q); sb("sz", C, _s)
+    sb("xh", 4 * C, _b); sb("zp", 4 * C, _b); sb("z", 4 * C, _b); sb("h", 4 * C, _b); sb("d", 4 * C, _b)
+    for r in range(3):
+        sb("za%d" % r, 36, _u); sb("zb%d" % r, 18, _u); sb("la%d" % r, 36, _u); sb("lb%d" % r, 18, _u)
+        sb("qh%d" % r, C, _q); sb("sh%d" % r, C, _s); sb("lq%d" % r, C, _q); sb("ls%d" % r, C, _s)
+    sb("yt", C, _f); sb("owt", 3 * C, _f)
+    d["ps"] = ("psum", [128, 4096], _f)
+    return d
+
+
+SCRATCH = _scratch()
+_DMAS = ["x", "u", "v", "w", "wc", "ws", "y0", "y1", "ow", "oc", "os0", "os1", "os2", "os3"]
+SEMAPHORES = (["qv", "qs", "qt", "qg", "loc"] + ["d" + n for n in _DMAS] +
+              ["r%s%d" % (n, r) for n in ("a", "b", "q0", "q1", "s0", "s1") for r in range(3)])
+
+
+def rank_program(g, core, T, topo):
+    rank = T.rank_of(core)
+    if rank is None:
+        return
+    queue = {"v": g.vector, "s": g.scalar, "t": g.tensor, "g": g, "y": g.sync}
+    count = {"v": 0, "s": 0, "t": 0, "g": 0}
+    known = {q: {} for q in queue}
+    snap, wrote, read, total, waited = {}, {}, {}, {}, {}
+
+    def before(q, rd, wr):
+        own = "q" + q
+        deps = set(wrote[k] for k in rd if k in wrote)
+        for k in wr:
+            deps |= set(w for w in [wrote.get(k)] + read.get(k, []) if w and w[0] != own)
+        best = {}
+        for s, n in deps:
+            if n > known[q].get(s, 0):
+                best[s] = max(n, best.get(s, 0))
+        for s, n in sorted(best.items()):
+            if any(o != s and snap.get((o, m), {}).get(s, 0) >= n for o, m in best.items()):
+                continue
+            queue[q].wait_ge(T.sem[s], n)
+            waited[s] = max(n, waited.get(s, 0))
+            known[q][s] = n
+            for o, m in snap.get((s, n), {}).items():
+                known[q][o] = max(m, known[q].get(o, 0))
+
+    def after(q, tag, rd, wr):
+        snap[tag] = dict(known[q])
+        total[tag[0]] = max(total.get(tag[0], 0), tag[1])
+        for k in rd:
+            read.setdefault(k, []).append(tag)
+        for k in wr:
+            wrote[k] = tag
+            read[k] = []
+
+    def op(q, fn, rd, wr):
+        before(q, rd, wr)
+        count[q] += 1
+        fn(queue[q]).then_inc(T.sem["q" + q], 1)
+        after(q, ("q" + q, count[q]), rd, wr)
+
+    def dma(q, name, out, in_, rd, wr):
+        before(q, rd, wr)
+        queue[q].dma_start(out, in_).then_inc(T.sem["d" + name], 16)
+        after(q, ("d" + name, 16), rd, wr)
+
+    def tt(out, a, b, o, rd, wr):
+        op("v", lambda e: e.tensor_tensor(out, a, b, o), rd, wr)
+
+    def ts(out, a, s1, o1, rd, wr, s2=None, o2=None):
+        if o2 is None:
+            op("v", lambda e: e.tensor_scalar(out, a, s1, None, o1), rd, wr)
+        else:
+            op("v", lambda e: e.tensor_scalar(out, a, s1, s2, o1, o2), rd, wr)
+
+    def cp(out, a, rd, wr):
+        op("v", lambda e: e.tensor_copy(out, a), rd, wr)
+
+    def fill(out, c, wr):
+        op("v", lambda e: e.memset(out, c), [], wr)
+
+    def ac(out, a, rd, wr, scale=1.0, bias=0.0, func=F.Copy):
+        op("s", lambda e: e.activation(out, a, func, bias=bias, scale=scale), rd, wr)
+
+    def scan(out, mask, v, rd, wr):
+        op("v", lambda e: e.tensor_tensor_scan(out, mask, v, 0.0, A.add, A.max), rd, wr)
+
+    def quant(q, s, x, rd, wr):
+        op("v", lambda e: e.quantize_mx(q, s, x), rd, wr)
+
+    def mm(bank, n, w, ws, x, xs, rd):
+        op("t", lambda e: e.matmul_mx(T.ps[:, 512 * bank:512 * bank + n], w, ws, x, xs, True, True), rd, ["b%d" % bank])
+
+    def bank(b, n=C):
+        return T.ps[:, 512 * b:512 * b + n]
+
+    def k18(k):
+        return slice(18 * k, 18 * k + 18)
+
+    def kc(k):
+        return slice(C * k, C * k + C)
+
+    dma("s", "w", T.wi[:], T.wl[:], [], ["wi"])
+    dma("y", "x", T.x0[:], T.x[:], [], ["x0.%d" % b for b in range(4)])
+    dma("s", "u", T.ut[:], T.u[:], [], ["ut"])
+    dma("y", "wc", T.wq[:, 0:512].bitcast(dt.uint8), T.wc[:, 0:2048], [], ["wq"])
+    dma("y", "ws", T.wsc[:, 0:512], T.ws[:, 0:512], [], ["wsc"])
+    dma("y", "v", T.vt[:], T.v[:], [], ["vt"])
+
+    def iota(out, pattern, base, cm, wr, small=False):
+        if small:
+            op("g", lambda e: e.iota(out, pattern, base, cm, allow_small_or_imprecise_dtypes=True), [], wr)
+        else:
+            op("g", lambda e: e.iota(out, pattern, base, cm), [], wr)
+    iota(T.ei[:], [[1, 16]], 128, -1, ["ei"])
+    iota(T.cr[:], [[1, C]], 0, 0, ["cr"], True)
+    iota(T.i1[:], [[0, 18]], 0, 1, ["i1"])
+    iota(T.i2[:], [[16, 18]], C, 0, ["i2"])
+    iota(T.ui[:], [[1, 2], [16, 8]], 0, 0, ["ui"])
+    fill(T.ones[:], 1.0, ["ones"])
+    op("g", lambda e: e.affine_select(T.ident[:], T.ones[:], [[-1, 128]], A.is_equal, 0.0, 0, 1), ["ones"], ["ident"])
+    fill(T.et[:], 0.0, ["et"])
+    fill(T.t3[:, 0:C], 0.0, ["t3a"])
+    fill(T.t3[:, C:2 * C], HUGE, ["t3b"])
+    ts(T.ea[:], T.ei[:], 15, A.bitwise_and, ["ei"], ["ea"])
+    ts(T.e0[:], T.ea[:], 0.0, A.is_equal, ["ea"], ["e0"], -4.0, A.mult)
+    ts(T.e1[:], T.ea[:], 1.0, A.is_equal, ["ea"], ["e1"], 2.0, A.mult)
+    ts(T.bp2[:, 0:1], T.ea[:, 15:16], 0.0, A.not_equal, ["ea"], ["bp2"], 2.0, A.mult)
+    ts(T.bpn[:, 0:1], T.ea[:, 15:16], 0.0, A.not_equal, ["ea"], ["bpn"], 2.0 * BIG, A.mult)
+    tt(T.mf[:, 0:16], T.e0[:], T.e1[:], A.add, ["e0", "e1"], ["mf"])
+    for n in (16, 32, 64, 128, 256):
+        m = min(n, C - n)
+        cp(T.mf[:, n:n + m], T.mf[:, 0:m], ["mf"], ["mf"])
+    for k in range(3):
+        ts(T.mn[:, kc(k)], T.mf[:], BIG, A.mult, ["mf"], ["mn"])
+    ts(T.i3[:], T.i1[:], 15, A.bitwise_and, ["i1"], ["i3"])
+    cp(T.uo[:], T.ui[:], ["ui"], ["uo"])
+    tt(T.cl[:], T.i3[:], T.i2[:], A.add, ["i3", "i2"], ["cl"])
+    bp2, bpn = T.bp2[:, 0:1], T.bpn[:, 0:1]
+    ac(T.t0[:, 0:C], T.cr[:], ["cr"], ["t0a"], 0.0, 512.0)
+    ac(T.t0[:, C:], T.cr[:], ["cr"], ["t0b"], 0.0, 2048.0 * 512)
+    ac(T.cr0[:], T.cr[:], ["cr"], ["cr0"], 2049.0)
+    ac(T.t1[:, 0:C], T.cr[:], ["cr"], ["t1a"], 2048.0, 1024.0 + 2048 * 512)
+    ac(T.t1[:, C:], T.cr[:], ["cr"], ["t1b"], 2048.0, 512.0)
+    ac(T.t2[:, 0:C], T.cr[:], ["cr"], ["t2a"], 2048.0, 2048.0 * 1024)
+    ac(T.t2[:, C:], T.cr[:], ["cr"], ["t2b"], 2048.0, 1024.0 + 2048 * 1024)
+    for k in range(2):
+        ac(T.pi[:, 512 * k + C:512 * k + 512], T.cr[:, 0:224], ["cr"], ["pig%d" % k])
+    for b in range(4):
+        ac(T.et[:, 512 * b + b:512 * b + 512:4], T.ident[:], ["ident", "et"], ["et%d" % b])
+    for k in range(2):
+        ac(T.zt[:, 512 * k + C:512 * k + 512], T.cr[:, 0:224], ["cr"], ["ztg%d" % k])
+
+    ts(T.c1[:], T.wi[:], float(C), A.is_ge, ["wi"], ["c1"], 224.0, A.mult)
+    ts(T.c2[:], T.wi[:], 2.0 * C, A.is_ge, ["wi"], ["c2"], 224.0, A.mult)
+    tt(T.c3[:], T.c1[:], T.wi[:], A.add, ["c1", "wi"], ["c3"])
+    tt(T.new0[:], T.c3[:], T.c2[:], A.add, ["c3", "c2"], ["new0.0", "new0.1", "new0.2"])
+
+    def lists(r):
+        w0 = T["new%d" % (r % 2)][:, 0:18]
+        w = "new%d.0" % (r % 2)
+        tt(T.tl[:], w0, T.cl[:], A.subtract, [w, "cl"], ["tl"])
+        ts(T.al[:], w0, 512.0, A.is_lt, [w], ["al"])
+        tt(T.tm[:], T.tl[:], T.al[:], A.mult, ["tl", "al"], ["tm"])
+        ts(T.qe[:, 0:18], T.al[:], 576.0, A.mult, ["al"], ["qe0"], -288.0, A.add)
+        tt(T.dp[:], T.tm[:], T.cl[:], A.add, ["tm", "cl"], ["dp"])
+        ts(T.qe[:, 18:36], T.al[:], 288.0, A.mult, ["al"], ["qe1"], 288.0, A.add)
+        cp(T.do[:], T.dp[:], ["dp"], ["do"])
+
+    def lists2():
+        tt(T.ie[:, 0:18], T.qe[:, 0:18], T.dp[:], A.add, ["qe0", "dp"], ["ie0"])
+        tt(T.ie[:, 18:36], T.qe[:, 18:36], T.dp[:], A.add, ["qe1", "dp"], ["ie1"])
+        cp(T.ieo[:], T.ie[:], ["ie0", "ie1"], ["ieo"])
+
+    def pis():
+        for k in range(3):
+            row = T.cr0 if k == 0 else T.cr
+            t = T["t%d" % k]
+            tt(T.pi[:, 512 * k:512 * k + C], t[:, 0:2 * C].indirect(T.do[:, 0:18]), row[:], A.add,
+               ["do", "t%da" % k, "t%db" % k, "cr0" if k == 0 else "cr"], ["pi%d" % k])
+
+    def thr():
+        ac(T.thr[:], T.t3[:, 0:2 * C].indirect(T.do[:, 0:18]), ["do", "t3a", "t3b"], ["thr"])
+
+    def nrow(r):
+        o = "off%d" % (r % 2)
+        ac(T.nr[:], T.pi[:, 0:1024 + C].indirect(T[o][:, 0:54]), ["pi0", "pi1", "pi2", "pig0", "pig1", o], ["nr"])
+
+    def erow():
+        ac(T.er[:], T.nr[:, 0:3 * C].indirect(T.ieo[:, 0:36]), ["nr", "ieo"], ["er"])
+
+    def prep1():
+        ns = T.ns
+        scan(T.ns[:], T.mn[:], T.nr[:], ["mn", "nr"], ["ns"])
+        tt(T.df[:, 18:54], ns[:, 15:576:16], ns[:, 303:864:16], A.subtract, ["ns"], ["df1"])
+        tt(T.df[:, 0:18], ns[:, 591:864:16], ns[:, 15:288:16], A.subtract, ["ns"], ["df0"])
+        for k in (1, 2, 0):
+            tt(T.dg[:, k18(k)], T.df[:, k18(k)], T.al[:], A.mult, ["df0" if k == 0 else "df1", "al"], ["dg%d" % k])
+        tt(T.base[:], T.dg[:], ns[:, 15:864:16], A.add, ["dg0", "dg1", "dg2", "ns"], ["base"])
+
+    def prep2():
+        es = T.es
+        scan(T.es[:], T.mn[:, 0:2 * C], T.er[:], ["mn", "er"], ["es"])
+        tt(T.dl[:, 0:18], T.base[:, 18:36], T.base[:, 0:18], A.subtract, ["base"], ["dl0"])
+        tt(T.dl[:, 18:54], es[:, 15:576:16], T.base[:, 18:54], A.subtract, ["es", "base"], ["dl1"])
+        ts(T.bd[:], T.dl[:], bp2, A.mult, ["dl0", "dl1", "bp2", "bpn"], ["bd"], bpn, A.add)
+        tt(T.base2[:], T.base[:], T.bd[:], A.subtract, ["base", "bd"], ["base2"])
+
+    def halves(r):
+        for b in range(4):
+            ac(T.xh[:, kc(b)], T["x%d" % r][:, b:4 * C:4], ["x%d.%d" % (r, b)], ["xh%d" % b], 0.5)
+
+    def qstate(r):
+        quant(T.qx[:, 0:C], T.sx[:, 0:C], T["x%d" % r][:, 0:4 * C], ["x%d.%d" % (r, b) for b in range(4)], ["qx"])
+
+    def scores():
+        for k in (1, 0):
+            mm(k, C, T.u2[:, 128 * k:128 * k + 128], T.u2s[:, 128 * k:128 * k + 128], T.qx[:, 0:C], T.sx[:, 0:C],
+               ["u2", "u2s", "qx"])
+
+    lists(0)
+    cp(T.off0[:], T.new0[:], ["new0.0", "new0.1", "new0.2"], ["off0"])
+    lists2()
+    thr()
+    quant(T.uq[:, 0:128], T.us[:, 0:128], T.ut[:, 0:512], ["ut"], ["uq"])
+    op("s", lambda e: e.activation(T.u2s[:, 0:256], T.us[:, 0:128].indirect(T.uo[:, 0:16]), F.Copy), ["uq", "uo"], ["u2s"])
+    pis()
+    nrow(0)
+    op("v", lambda e: e.tensor_copy(T.u2[:, 0:256].bitcast(dt.uint32), T.uq[:, 0:128].bitcast(dt.uint32).indirect(T.uo[:, 0:16])),
+       ["uq", "uo"], ["u2"])
+    qstate(0)
+    scores()
+    erow()
+    prep1()
+    quant(T.eq[:, 0:512], T.esc[:, 0:512], T.et[:, 0:2048], ["et%d" % b for b in range(4)], ["eq"])
+    prep2()
+
+    for r in range(3):
+        peer = T.cores[rank ^ STEP[r]]
+        rid, pid = topo.addr(peer, core)
+        mask = topo.mask(core, peer)
+        arrive = len(topo.engines(peer, core))
+        last = r == 2
+
+        def send(dst, src, sem, rd):
+            before("g", rd, [])
+            g.remote_dma(out_ap=dst, in_ap=src, remote_sem=T.sem[sem], local_sem=T.sem.loc, pid=pid, routing_id=rid,
+                         dma_engine_mask=mask)
+            total["loc"] = total.get("loc", 0) + len(topo.engines(core, peer))
+
+        def arrival(sem, key):
+            wrote[key] = (sem, arrive)
+            snap[(sem, arrive)] = {}
+            total[sem] = arrive
+        arrival("ra%d" % r, "la")
+        arrival("rb%d" % r, "lb")
+        for i in range(2):
+            arrival("rq%d%d" % (i, r), "lq%d" % i)
+            arrival("rs%d%d" % (i, r), "ls%d" % i)
+        n = (r + 1) % 2
+        new, off, za, zb = T["new%d" % n], T["off%d" % n], T["za%d" % r], T["zb%d" % r]
+        lq, ls, qh, sh = T["lq%d" % r], T["ls%d" % r], T["qh%d" % r], T["sh%d" % r]
+
+        ac(T.a2[:, C:2 * C], bank(1), ["b1"], ["a2b"], func=F.Relu)
+        tt(T.am[:], bank(0), T.thr[:], A.is_gt, ["b0", "thr"], ["am"])
+        cp(T.a2[:, 0:C], T.am[:], ["am"], ["a2a"])
+        halves(r)
+        tt(T.fr[:], T.a2[:, 0:2 * C].indirect(T.do[:, 0:18]), T.am[:], A.not_equal, ["a2a", "a2b", "am", "do"], ["fr"])
+        scan(T.fs[:], T.mf[:], T.fr[:], ["mf", "fr"], ["fs"])
+
+        for k in (1, 2, 0):
+            tt(T.st[:, k18(k)], T.fs[:, 15:C:16], T.dl[:, k18(k)], A.mult, ["fs", "dl0", "dl1"], ["st%d" % k])
+        tt(T.sel[:], T.st[:], T.base2[:], A.add, ["st0", "st1", "st2", "base2"], ["sel"])
+        ts(T.xi[:], T.sel[:], 511, A.bitwise_and, ["sel"], ["xi"])
+        cp(T.xo[:], T.xi[:], ["xi"], ["xo"])
+        for k in (1, 2):
+            ac(T.fx[:, kc(k)], T.fr[:, 0:C].indirect(T.xo[:, k18(k)]), ["fr", "xo"], ["fx%d" % k])
+        ts(T.n0[:], T.sel[:], 2047, A.bitwise_and, ["sel"], ["n0"])
+        ts(T.n1[:], T.sel[:], 11, A.logical_shift_right, ["sel"], ["n1"])
+        tt(T.dn[:], T.n1[:], T.n0[:], A.subtract, ["n1", "n0"], ["dn"])
+        ts(T.bb[:], T.dn[:], bp2, A.mult, ["dn", "bp2"], ["bb"])
+        tt(T.b2[:], T.n0[:], T.bb[:], A.subtract, ["n0", "bb"], ["b2"])
+
+        def ports_a(k):
+            s = k18(k)
+            scan(T.fxs[:, kc(k)], T.mf[:], T.fx[:, kc(k)], ["mf", "fx%d" % k], ["fxs%d" % k])
+            tt(T.nt[:, s], T.fxs[:, C * k + 15:C * k + C:16], T.dn[:, s], A.mult, ["fxs%d" % k, "dn"], ["nt%d" % k])
+            tt(new[:, s], T.nt[:, s], T.b2[:, s], A.add, ["nt%d" % k, "b2"], ["new%d.%d" % (n, k)])
+
+        def ports_b(k):
+            s = k18(k)
+            z = zb[:] if k == 0 else za[:, k18(k - 1)]
+            ts(T.zi[:, s], new[:, s], 511, A.bitwise_and, ["new%d.%d" % (n, k)], ["zi%d" % k])
+            cp(z, T.zi[:, s], ["zi%d" % k], ["zo%d" % k])
+        for k in (1, 2):
+            ports_a(k)
+            ports_b(k)
+        send(T["la%d" % r][:], za[:], "ra%d" % r, ["zo1", "zo2"])
+
+        def hquant(i):
+            a, e = CUT[i]
+            quant(qh[:, a:e], sh[:, a:e], T.h[:, 4 * a:4 * e], ["h%d%d" % (i, b) for b in range(4)], ["qh%d" % i])
+            send(lq[:, a:e].bitcast(dt.uint8), qh[:, a:e].bitcast(dt.uint8), "rq%d%d" % (i, r), ["qh%d" % i])
+            send(ls[:, a:e], sh[:, a:e], "rs%d%d" % (i, r), ["qh%d" % i])
+        for i, (a, e) in enumerate(CUT):
+            for b in range(4):
+                ac(T.zp[:, C * b + a:C * b + e], T.xh[:, kc(b)].indirect(za[:, a // 16:e // 16]),
+                   ["xh%d" % b, "zo1"], ["zp%d%d" % (i, b)])
+                tt(T.z[:, 4 * a + b:4 * e:4], T.xh[:, kc(b)].indirect(za[:, 18 + a // 16:18 + e // 16]),
+                   T.zp[:, C * b + a:C * b + e], A.add, ["xh%d" % b, "zo2", "zp%d%d" % (i, b)], ["z%d" % i])
+            if i == 0:
+                ac(T.fx[:, 0:C], T.fr[:, 0:C].indirect(T.xo[:, 0:18]), ["fr", "xo"], ["fx0"])
+            quant(T.qz[:, a:e], T.sz[:, a:e], T.z[:, 4 * a:4 * e], ["z%d" % i], ["qz%d" % i])
+        for i, (a, e) in enumerate(CUT):
+            for b in range(4):
+                k = (2 + 4 * i + b) % 8
+                mm(k, e - a, T.wq[:, 128 * b:128 * b + 128], T.wsc[:, 128 * b:128 * b + 128], T.qz[:, a:e], T.sz[:, a:e],
+                   ["wq", "wsc", "qz%d" % i])
+                ac(T.h[:, 4 * a + b:4 * e:4], bank(k, e - a), ["b%d" % k], ["h%d%d" % (i, b)], 0.03125)
+        ports_a(0)
+        hquant(0)
+        ports_b(0)
+        send(T["lb%d" % r][:], zb[:], "rb%d" % r, ["zo0"])
+        cp(off[:], new[:], ["new%d.%d" % (n, k) for k in range(3)], ["off%d" % n])
+        hquant(1)
+
+        if r == 0:
+            iota(T.pt[:], [[C, 3], [1, 512]], 0, 0, ["pt"], True)
+        if not last:
+            lists(r + 1)
+            pis()
+            lists2()
+            thr()
+        for k in (1, 2):
+            ac(T.zt[:, 512 * k:512 * k + C], T.cr[:, 0:C].indirect(T["la%d" % r][:, k18(k - 1)]), ["cr", "la"], ["zt%d" % k])
+        if last:
+            quant(T.vq[:, 0:128], T.vs[:, 0:128], T.vt[:, 0:512], ["vt"], ["vq"])
+        cp(T.zt[:, 0:C], T.cr[:, 0:C].indirect(T["lb%d" % r][:, 0:18]), ["cr", "lb"], ["zt0"])
+        if not last:
+            nrow(r + 1)
+        ac(T.mr[:], T.zt[:, 0:1024 + C].indirect(off[:, 0:18]), ["zt0", "zt1", "zt2", "ztg0", "ztg1", "off%d" % n], ["mr"])
+        if not last:
+            prep1()
+        scan(T.ms[:], T.mn[:, 0:C], T.mr[:], ["mn", "mr"], ["ms"])
+        ts(T.mo[:], T.ms[:, 15:C:16], bpn, A.subtract, ["ms", "bpn"], ["mo"])
+        if last:
+            ac(T.owt[:], T.pt[:, 0:1024 + C].indirect(off[:, 0:54]), ["pt", "off%d" % n], ["owt"])
+            dma("y", "ow", T.ow[:], T.owt[0:128:16, :], ["owt"], [])
+
+        x, y = "x%d" % r, "x%d" % (r + 1)
+        for i, (a, e) in enumerate(CUT):
+            for b in range(4):
+                k = (2 + 4 * i + b) % 8
+                mm(k, e - a, T.eq[:, 128 * b:128 * b + 128], T.esc[:, 128 * b:128 * b + 128], lq[:, a:e], ls[:, a:e],
+                   ["eq", "lq%d" % i, "ls%d" % i])
+                ac(T.d[:, C * b + a:C * b + e], bank(k, e - a), ["b%d" % k], ["d%d%d" % (i, b)])
+        if not last:
+            erow()
+        for b in range(4):
+            tt(T[y][:, b:4 * C:4], T.d[:, kc(b)].indirect(T.mo[:, 0:18]), T[x][:, b:4 * C:4], A.add,
+               ["d0%d" % b, "d1%d" % b, "mo", "%s.%d" % (x, b)], ["%s.%d" % (y, b)])
+        qstate(r + 1)
+        if not last:
+            scores()
+            prep2()
+
+    h = C // 2
+    for i in range(2):
+        mm(2 + i, h, T.vq[:, 0:128], T.vs[:, 0:128], T.qx[:, h * i:h * i + h], T.sx[:, h * i:h * i + h], ["vq", "qx"])
+    dma("y", "oc", T.oc[:, 0:4 * C], T.qx[:, 0:C].bitcast(dt.uint8), ["qx"], [])
+    for k in range(4):
+        dma("y", "os%d" % k, T.osc[4 * k:4 * k + 4, 0:C], T.sx[32 * k:32 * k + 4, 0:C], ["qx"], [])
+    cp(T.yt[:, h:C], bank(3, h), ["b3"], ["yt1"])
+    ac(T.yt[:, 0:h], bank(2, h), ["b2"], ["yt0"])
+    dma("s", "y0", T.y[:, 0:h], T.yt[:, 0:h], ["yt0"], [])
+    dma("s", "y1", T.y[:, h:C], T.yt[:, h:C], ["yt1"], [])
+    for s, m in sorted(total.items()):
+        if waited.get(s, 0) < m:
+            g.wait_ge(T.sem[s], m)

@@ -19,13 +19,13 @@ def _scratch():
     sb("wq", 512, _q); sb("wsc", 512, _s)
     sb("uq", 128, _q); sb("us", 128, _s); sb("u2", 256, _q); sb("u2s", 256, _s)
     sb("vq", 128, _q); sb("vs", 128, _s)
-    sb("ident", 128, _b); sb("ones", 128, _b); sb("et", 2048, _b); sb("eq", 512, _q); sb("esc", 512, _s)
+    sb("ones", 512, _b); sb("et", 2048, _b); sb("eq", 512, _q); sb("esc", 512, _s)
     sb("cr", C, _f); sb("cr0", C, _f); sb("t0", 2 * C, _f); sb("t1", 2 * C, _f); sb("t2", 2 * C, _f); sb("t3", 2 * C, _b)
     sb("ei", 16, _i); sb("ea", 16, _i); sb("e0", 16, _b); sb("e1", 16, _b); sb("mf", C, _b); sb("mn", 3 * C, _b)
     sb("bp2", 8, _f); sb("bpn", 8, _f)
     sb("i1", 18, _i); sb("i2", 18, _i); sb("i3", 18, _i); sb("cl", 18, _f); sb("ui", 16, _i); sb("uo", 16, _u)
     sb("pt", 1536, _f)
-    sb("c1", 54, _f); sb("c2", 54, _f); sb("c3", 54, _f)
+    sb("c1", 54, _f); sb("c2", 54, _f)
     for r in range(2):
         sb("new%d" % r, 54, _i); sb("off%d" % r, 54, _u)
     sb("al", 18, _f); sb("tl", 18, _f); sb("tm", 18, _f); sb("dp", 18, _f); sb("do", 18, _u)
@@ -35,7 +35,8 @@ def _scratch():
     sb("a2", 2 * C, _b); sb("am", C, _b); sb("fr", C, _b); sb("fs", C, _b)
     sb("st", 54, _f); sb("sel", 54, _i); sb("xi", 54, _i); sb("xo", 54, _u)
     sb("n0", 54, _i); sb("n1", 54, _i); sb("dn", 54, _f); sb("bb", 54, _f); sb("b2", 54, _f)
-    sb("fx", 3 * C, _b); sb("fxs", 3 * C, _b); sb("nt", 54, _f); sb("zi", 54, _i)
+    sb("fx", 3 * C, _b); sb("fxs", 3 * C, _b); sb("nt", 54, _f)
+    sb("zn", 54, _i); sb("dz", 54, _f); sb("bz", 54, _f); sb("zf", 54, _f)
     sb("zt", 1536, _f); sb("mr", C, _f); sb("ms", C, _f); sb("mo", 18, _u)
     for r in range(4):
         sb("x%d" % r, 4 * C, _b)
@@ -52,7 +53,7 @@ def _scratch():
 SCRATCH = _scratch()
 _DMAS = ["x", "u", "v", "w", "wc", "ws", "y0", "y1", "ow", "oc", "os0", "os1", "os2", "os3"]
 SEMAPHORES = (["qv", "qs", "qt", "qg", "loc"] + ["d" + n for n in _DMAS] +
-              ["r%s%d" % (n, r) for n in ("a", "b", "q0", "q1", "s0", "s1") for r in range(3)])
+              ["r%s%d" % (n, r) for n in ("a", "b", "q0", "q1", "s") for r in range(3)])
 
 
 def rank_program(g, core, T, topo):
@@ -155,9 +156,10 @@ def rank_program(g, core, T, topo):
     iota(T.i1[:], [[0, 18]], 0, 1, ["i1"])
     iota(T.i2[:], [[16, 18]], C, 0, ["i2"])
     iota(T.ui[:], [[1, 2], [16, 8]], 0, 0, ["ui"])
-    fill(T.ones[:], 1.0, ["ones"])
-    op("g", lambda e: e.affine_select(T.ident[:], T.ones[:], [[-1, 128]], A.is_equal, 0.0, 0, 1), ["ones"], ["ident"])
-    fill(T.et[:], 0.0, ["et"])
+    iota(T.ones[:], [[0, 512]], 1, 0, ["ones"], True)
+    for b in range(4):
+        op("g", lambda e: e.affine_select(T.et[:, 512 * b:512 * b + 512], T.ones[:], [[-1, 512]], A.is_equal, 0.0, b, 4),
+           ["ones"], ["et%d" % b])
     fill(T.t3[:, 0:C], 0.0, ["t3a"])
     fill(T.t3[:, C:2 * C], HUGE, ["t3b"])
     ts(T.ea[:], T.ei[:], 15, A.bitwise_and, ["ei"], ["ea"])
@@ -184,19 +186,17 @@ def rank_program(g, core, T, topo):
     ac(T.t2[:, C:], T.cr[:], ["cr"], ["t2b"], 2048.0, 1024.0 + 2048 * 1024)
     for k in range(2):
         ac(T.pi[:, 512 * k + C:512 * k + 512], T.cr[:, 0:224], ["cr"], ["pig%d" % k])
-    for b in range(4):
-        ac(T.et[:, 512 * b + b:512 * b + 512:4], T.ident[:], ["ident", "et"], ["et%d" % b])
     for k in range(2):
         ac(T.zt[:, 512 * k + C:512 * k + 512], T.cr[:, 0:224], ["cr"], ["ztg%d" % k])
 
     ts(T.c1[:], T.wi[:], float(C), A.is_ge, ["wi"], ["c1"], 224.0, A.mult)
     ts(T.c2[:], T.wi[:], 2.0 * C, A.is_ge, ["wi"], ["c2"], 224.0, A.mult)
-    tt(T.c3[:], T.c1[:], T.wi[:], A.add, ["c1", "wi"], ["c3"])
-    tt(T.new0[:], T.c3[:], T.c2[:], A.add, ["c3", "c2"], ["new0.0", "new0.1", "new0.2"])
+    tt(T.c1[:], T.c1[:], T.wi[:], A.add, ["c1", "wi"], ["c3"])
+    tt(T.new0[:], T.c1[:], T.c2[:], A.add, ["c3", "c2"], ["new0"])
 
     def lists(r):
         w0 = T["new%d" % (r % 2)][:, 0:18]
-        w = "new%d.0" % (r % 2)
+        w = "new%d" % (r % 2)
         tt(T.tl[:], w0, T.cl[:], A.subtract, [w, "cl"], ["tl"])
         ts(T.al[:], w0, 512.0, A.is_lt, [w], ["al"])
         tt(T.tm[:], T.tl[:], T.al[:], A.mult, ["tl", "al"], ["tm"])
@@ -222,27 +222,23 @@ def rank_program(g, core, T, topo):
 
     def nrow(r):
         o = "off%d" % (r % 2)
-        ac(T.nr[:], T.pi[:, 0:1024 + C].indirect(T[o][:, 0:54]), ["pi0", "pi1", "pi2", "pig0", "pig1", o], ["nr"])
+        rd = ["pi0", "pi1", "pi2", "pig0", "pig1", o]
+        ac(T.nr[:, 0:2 * C], T.pi[:, 0:1024 + C].indirect(T[o][:, 0:36]), rd, ["nr0"])
+        cp(T.nr[:, 2 * C:3 * C], T.pi[:, 0:1024 + C].indirect(T[o][:, 36:54]), rd, ["nr1"])
 
     def erow():
-        ac(T.er[:], T.nr[:, 0:3 * C].indirect(T.ieo[:, 0:36]), ["nr", "ieo"], ["er"])
+        ac(T.er[:], T.nr[:, 0:3 * C].indirect(T.ieo[:, 0:36]), ["nr0", "nr1", "ieo"], ["er"])
 
     def prep1():
         ns = T.ns
-        scan(T.ns[:], T.mn[:], T.nr[:], ["mn", "nr"], ["ns"])
+        scan(T.ns[:], T.mn[:], T.nr[:], ["mn", "nr0", "nr1"], ["ns"])
         tt(T.df[:, 18:54], ns[:, 15:576:16], ns[:, 303:864:16], A.subtract, ["ns"], ["df1"])
         tt(T.df[:, 0:18], ns[:, 591:864:16], ns[:, 15:288:16], A.subtract, ["ns"], ["df0"])
         for k in (1, 2, 0):
             tt(T.dg[:, k18(k)], T.df[:, k18(k)], T.al[:], A.mult, ["df0" if k == 0 else "df1", "al"], ["dg%d" % k])
-        tt(T.base[:], T.dg[:], ns[:, 15:864:16], A.add, ["dg0", "dg1", "dg2", "ns"], ["base"])
 
-    def prep2():
-        es = T.es
-        scan(T.es[:], T.mn[:, 0:2 * C], T.er[:], ["mn", "er"], ["es"])
-        tt(T.dl[:, 0:18], T.base[:, 18:36], T.base[:, 0:18], A.subtract, ["base"], ["dl0"])
-        tt(T.dl[:, 18:54], es[:, 15:576:16], T.base[:, 18:54], A.subtract, ["es", "base"], ["dl1"])
-        ts(T.bd[:], T.dl[:], bp2, A.mult, ["dl0", "dl1", "bp2", "bpn"], ["bd"], bpn, A.add)
-        tt(T.base2[:], T.base[:], T.bd[:], A.subtract, ["base", "bd"], ["base2"])
+    def base():
+        tt(T.base[:], T.dg[:], T.ns[:, 15:864:16], A.add, ["dg0", "dg1", "dg2", "ns"], ["base"])
 
     def halves(r):
         for b in range(4):
@@ -257,7 +253,7 @@ def rank_program(g, core, T, topo):
                ["u2", "u2s", "qx"])
 
     lists(0)
-    cp(T.off0[:], T.new0[:], ["new0.0", "new0.1", "new0.2"], ["off0"])
+    cp(T.off0[:], T.new0[:], ["new0"], ["off0"])
     lists2()
     thr()
     quant(T.uq[:, 0:128], T.us[:, 0:128], T.ut[:, 0:512], ["ut"], ["uq"])
@@ -270,8 +266,7 @@ def rank_program(g, core, T, topo):
     scores()
     erow()
     prep1()
-    quant(T.eq[:, 0:512], T.esc[:, 0:512], T.et[:, 0:2048], ["et%d" % b for b in range(4)], ["eq"])
-    prep2()
+    base()
 
     for r in range(3):
         peer = T.cores[rank ^ STEP[r]]
@@ -294,15 +289,20 @@ def rank_program(g, core, T, topo):
         arrival("rb%d" % r, "lb")
         for i in range(2):
             arrival("rq%d%d" % (i, r), "lq%d" % i)
-            arrival("rs%d%d" % (i, r), "ls%d" % i)
+        arrival("rs%d" % r, "ls")
         n = (r + 1) % 2
         new, off, za, zb = T["new%d" % n], T["off%d" % n], T["za%d" % r], T["zb%d" % r]
         lq, ls, qh, sh = T["lq%d" % r], T["ls%d" % r], T["qh%d" % r], T["sh%d" % r]
 
         ac(T.a2[:, C:2 * C], bank(1), ["b1"], ["a2b"], func=F.Relu)
-        tt(T.am[:], bank(0), T.thr[:], A.is_gt, ["b0", "thr"], ["am"])
-        cp(T.a2[:, 0:C], T.am[:], ["am"], ["a2a"])
         halves(r)
+        scan(T.es[:], T.mn[:, 0:2 * C], T.er[:], ["mn", "er"], ["es"])
+        tt(T.am[:], bank(0), T.thr[:], A.is_gt, ["b0", "thr"], ["am"])
+        tt(T.dl[:, 18:54], T.es[:, 15:576:16], T.base[:, 18:54], A.subtract, ["es", "base"], ["dl1"])
+        tt(T.dl[:, 0:18], T.base[:, 18:36], T.base[:, 0:18], A.subtract, ["base"], ["dl0"])
+        cp(T.a2[:, 0:C], T.am[:], ["am"], ["a2a"])
+        ts(T.bd[:], T.dl[:], bp2, A.mult, ["dl0", "dl1", "bp2", "bpn"], ["bd"], bpn, A.add)
+        tt(T.base2[:], T.base[:], T.bd[:], A.subtract, ["base", "bd"], ["base2"])
         tt(T.fr[:], T.a2[:, 0:2 * C].indirect(T.do[:, 0:18]), T.am[:], A.not_equal, ["a2a", "a2b", "am", "do"], ["fr"])
         scan(T.fs[:], T.mf[:], T.fr[:], ["mf", "fr"], ["fs"])
 
@@ -311,43 +311,46 @@ def rank_program(g, core, T, topo):
         tt(T.sel[:], T.st[:], T.base2[:], A.add, ["st0", "st1", "st2", "base2"], ["sel"])
         ts(T.xi[:], T.sel[:], 511, A.bitwise_and, ["sel"], ["xi"])
         cp(T.xo[:], T.xi[:], ["xi"], ["xo"])
-        for k in (1, 2):
+        for k in (1, 2, 0):
             ac(T.fx[:, kc(k)], T.fr[:, 0:C].indirect(T.xo[:, k18(k)]), ["fr", "xo"], ["fx%d" % k])
-        ts(T.n0[:], T.sel[:], 2047, A.bitwise_and, ["sel"], ["n0"])
-        ts(T.n1[:], T.sel[:], 11, A.logical_shift_right, ["sel"], ["n1"])
-        tt(T.dn[:], T.n1[:], T.n0[:], A.subtract, ["n1", "n0"], ["dn"])
-        ts(T.bb[:], T.dn[:], bp2, A.mult, ["dn", "bp2"], ["bb"])
-        tt(T.b2[:], T.n0[:], T.bb[:], A.subtract, ["n0", "bb"], ["b2"])
+        ts(T.zn[:], T.sel[:], 11, A.logical_shift_right, ["sel"], ["zn"], 511, A.bitwise_and)
+        tt(T.dz[:], T.zn[:], T.xi[:], A.subtract, ["zn", "xi"], ["dz"])
+        ts(T.bb[:], T.dz[:], bp2, A.mult, ["dz", "bp2"], ["bb"])
+        tt(T.bz[:], T.xi[:], T.bb[:], A.subtract, ["xi", "bb"], ["bz"])
 
-        def ports_a(k):
-            s = k18(k)
+        def fscan(k):
             scan(T.fxs[:, kc(k)], T.mf[:], T.fx[:, kc(k)], ["mf", "fx%d" % k], ["fxs%d" % k])
-            tt(T.nt[:, s], T.fxs[:, C * k + 15:C * k + C:16], T.dn[:, s], A.mult, ["fxs%d" % k, "dn"], ["nt%d" % k])
-            tt(new[:, s], T.nt[:, s], T.b2[:, s], A.add, ["nt%d" % k, "b2"], ["new%d.%d" % (n, k)])
 
-        def ports_b(k):
-            s = k18(k)
-            z = zb[:] if k == 0 else za[:, k18(k - 1)]
-            ts(T.zi[:, s], new[:, s], 511, A.bitwise_and, ["new%d.%d" % (n, k)], ["zi%d" % k])
-            cp(z, T.zi[:, s], ["zi%d" % k], ["zo%d" % k])
-        for k in (1, 2):
-            ports_a(k)
-            ports_b(k)
+        def zmul(k):
+            tt(T.zf[:, k18(k)], T.fxs[:, C * k + 15:C * k + C:16], T.dz[:, k18(k)], A.mult, ["fxs%d" % k, "dz"], ["zm%d" % k])
+
+        def zadd(k):
+            tt(T.zf[:, k18(k)], T.zf[:, k18(k)], T.bz[:, k18(k)], A.add, ["zm%d" % k, "bz"], ["zf%d" % k])
+
+        def zout(k):
+            cp(zb[:] if k == 0 else za[:, k18(k - 1)], T.zf[:, k18(k)], ["zf%d" % k], ["zo%d" % k])
+        fscan(1)
+        zmul(1)
+        fscan(2)
+        zadd(1)
+        zmul(2)
+        zout(1)
+        zadd(2)
+        zout(2)
         send(T["la%d" % r][:], za[:], "ra%d" % r, ["zo1", "zo2"])
 
         def hquant(i):
             a, e = CUT[i]
             quant(qh[:, a:e], sh[:, a:e], T.h[:, 4 * a:4 * e], ["h%d%d" % (i, b) for b in range(4)], ["qh%d" % i])
             send(lq[:, a:e].bitcast(dt.uint8), qh[:, a:e].bitcast(dt.uint8), "rq%d%d" % (i, r), ["qh%d" % i])
-            send(ls[:, a:e], sh[:, a:e], "rs%d%d" % (i, r), ["qh%d" % i])
+            if i == 1:
+                send(ls[:, 0:C], sh[:, 0:C], "rs%d" % r, ["qh0", "qh1"])
         for i, (a, e) in enumerate(CUT):
             for b in range(4):
                 ac(T.zp[:, C * b + a:C * b + e], T.xh[:, kc(b)].indirect(za[:, a // 16:e // 16]),
                    ["xh%d" % b, "zo1"], ["zp%d%d" % (i, b)])
                 tt(T.z[:, 4 * a + b:4 * e:4], T.xh[:, kc(b)].indirect(za[:, 18 + a // 16:18 + e // 16]),
                    T.zp[:, C * b + a:C * b + e], A.add, ["xh%d" % b, "zo2", "zp%d%d" % (i, b)], ["z%d" % i])
-            if i == 0:
-                ac(T.fx[:, 0:C], T.fr[:, 0:C].indirect(T.xo[:, 0:18]), ["fr", "xo"], ["fx0"])
             quant(T.qz[:, a:e], T.sz[:, a:e], T.z[:, 4 * a:4 * e], ["z%d" % i], ["qz%d" % i])
         for i, (a, e) in enumerate(CUT):
             for b in range(4):
@@ -355,12 +358,21 @@ def rank_program(g, core, T, topo):
                 mm(k, e - a, T.wq[:, 128 * b:128 * b + 128], T.wsc[:, 128 * b:128 * b + 128], T.qz[:, a:e], T.sz[:, a:e],
                    ["wq", "wsc", "qz%d" % i])
                 ac(T.h[:, 4 * a + b:4 * e:4], bank(k, e - a), ["b%d" % k], ["h%d%d" % (i, b)], 0.03125)
-        ports_a(0)
+        fscan(0)
+        ts(T.n0[:], T.sel[:], 2047, A.bitwise_and, ["sel"], ["n0"])
+        ts(T.n1[:], T.sel[:], 11, A.logical_shift_right, ["sel"], ["n1"])
+        zmul(0)
+        tt(T.dn[:], T.n1[:], T.n0[:], A.subtract, ["n1", "n0"], ["dn"])
         hquant(0)
-        ports_b(0)
+        zadd(0)
+        ts(T.bb[:], T.dn[:], bp2, A.mult, ["dn", "bp2"], ["bb"])
+        tt(T.nt[:], T.fxs[:, 15:3 * C:16], T.dn[:], A.mult, ["fxs0", "fxs1", "fxs2", "dn"], ["nt"])
+        zout(0)
         send(T["lb%d" % r][:], zb[:], "rb%d" % r, ["zo0"])
-        cp(off[:], new[:], ["new%d.%d" % (n, k) for k in range(3)], ["off%d" % n])
+        tt(T.b2[:], T.n0[:], T.bb[:], A.subtract, ["n0", "bb"], ["b2"])
         hquant(1)
+        tt(new[:], T.nt[:], T.b2[:], A.add, ["nt", "b2"], ["new%d" % n])
+        cp(off[:], new[:], ["new%d" % n], ["off%d" % n])
 
         if r == 0:
             iota(T.pt[:], [[C, 3], [1, 512]], 0, 0, ["pt"], True)
@@ -371,36 +383,38 @@ def rank_program(g, core, T, topo):
             thr()
         for k in (1, 2):
             ac(T.zt[:, 512 * k:512 * k + C], T.cr[:, 0:C].indirect(T["la%d" % r][:, k18(k - 1)]), ["cr", "la"], ["zt%d" % k])
+        if r == 0:
+            quant(T.eq[:, 0:512], T.esc[:, 0:512], T.et[:, 0:2048], ["et%d" % b for b in range(4)], ["eq"])
         if last:
             quant(T.vq[:, 0:128], T.vs[:, 0:128], T.vt[:, 0:512], ["vt"], ["vq"])
-        cp(T.zt[:, 0:C], T.cr[:, 0:C].indirect(T["lb%d" % r][:, 0:18]), ["cr", "lb"], ["zt0"])
         if not last:
             nrow(r + 1)
+        ac(T.zt[:, 0:C], T.cr[:, 0:C].indirect(T["lb%d" % r][:, 0:18]), ["cr", "lb"], ["zt0"])
         ac(T.mr[:], T.zt[:, 0:1024 + C].indirect(off[:, 0:18]), ["zt0", "zt1", "zt2", "ztg0", "ztg1", "off%d" % n], ["mr"])
         if not last:
             prep1()
         scan(T.ms[:], T.mn[:, 0:C], T.mr[:], ["mn", "mr"], ["ms"])
+        if not last:
+            base()
         ts(T.mo[:], T.ms[:, 15:C:16], bpn, A.subtract, ["ms", "bpn"], ["mo"])
         if last:
             ac(T.owt[:], T.pt[:, 0:1024 + C].indirect(off[:, 0:54]), ["pt", "off%d" % n], ["owt"])
             dma("y", "ow", T.ow[:], T.owt[0:128:16, :], ["owt"], [])
 
         x, y = "x%d" % r, "x%d" % (r + 1)
-        for i, (a, e) in enumerate(CUT):
-            for b in range(4):
-                k = (2 + 4 * i + b) % 8
-                mm(k, e - a, T.eq[:, 128 * b:128 * b + 128], T.esc[:, 128 * b:128 * b + 128], lq[:, a:e], ls[:, a:e],
-                   ["eq", "lq%d" % i, "ls%d" % i])
-                ac(T.d[:, C * b + a:C * b + e], bank(k, e - a), ["b%d" % k], ["d%d%d" % (i, b)])
+        for b in range(4):
+            k = 2 + b
+            mm(k, C, T.eq[:, 128 * b:128 * b + 128], T.esc[:, 128 * b:128 * b + 128], lq[:, 0:C], ls[:, 0:C],
+               ["eq", "lq0", "lq1", "ls"])
+            ac(T.d[:, kc(b)], bank(k), ["b%d" % k], ["d%d" % b])
         if not last:
             erow()
         for b in range(4):
             tt(T[y][:, b:4 * C:4], T.d[:, kc(b)].indirect(T.mo[:, 0:18]), T[x][:, b:4 * C:4], A.add,
-               ["d0%d" % b, "d1%d" % b, "mo", "%s.%d" % (x, b)], ["%s.%d" % (y, b)])
+               ["d%d" % b, "mo", "%s.%d" % (x, b)], ["%s.%d" % (y, b)])
         qstate(r + 1)
         if not last:
             scores()
-            prep2()
 
     h = C // 2
     for i in range(2):

from concourse.mybir import dt, AluOpType as A, ActivationFunctionType as F

C = 288
STEP = [4, 1, 2]
HUGE = 1e29
BIG = 2097152.0
CUT = [(0, 160), (160, 288)]

_f, _b, _i, _u = "float32", "bfloat16", "int32", "uint16"
_q, _s = "float8_e4m3fn_x4", "uint8"


def _scratch():
    d = {}

    def sb(name, n, t):
        d[name] = ("sbuf", [128, n], t)
    sb("ut", 512, _b); sb("vt", 512, _b); sb("wi", 54, _i)
    sb("wq", 512, _q); sb("wsc", 512, _s)
    sb("uq", 128, _q); sb("us", 128, _s); sb("u2", 256, _q); sb("u2s", 256, _s)
    sb("vq", 128, _q); sb("vs", 128, _s)
    sb("ones", 512, _b); sb("et", 2048, _b); sb("eq", 512, _q); sb("esc", 512, _s)
    sb("cr", C, _f); sb("cr0", C, _f); sb("t0", 2 * C, _f); sb("t1", 2 * C, _f); sb("t2", 2 * C, _f); sb("t3", 2 * C, _b)
    sb("ei", 16, _i); sb("ea", 16, _i); sb("e0", 16, _b); sb("e1", 16, _b); sb("mf", C, _b); sb("mn", 3 * C, _b)
    sb("bp2", 8, _f); sb("bpn", 8, _f)
    sb("i1", 18, _i); sb("i2", 18, _i); sb("i3", 18, _i); sb("cl", 18, _f); sb("ui", 16, _i); sb("uo", 16, _u)
    sb("pt", 1536, _f)
    sb("c1", 54, _f); sb("c2", 54, _f)
    for r in range(2):
        sb("new%d" % r, 54, _i); sb("off%d" % r, 54, _u)
    sb("al", 18, _f); sb("tl", 18, _f); sb("tm", 18, _f); sb("dp", 18, _f); sb("do", 18, _u)
    sb("qe", 36, _f); sb("ie", 36, _f); sb("ieo", 36, _u)
    sb("pi", 1536, _f); sb("thr", C, _b); sb("nr", 3 * C, _f); sb("ns", 3 * C, _f); sb("er", 2 * C, _f); sb("es", 2 * C, _f)
    sb("df", 54, _f); sb("dg", 54, _f); sb("base", 54, _f); sb("dl", 54, _f); sb("bd", 54, _f); sb("base2", 54, _f)
    sb("a2", 2 * C, _b); sb("am", C, _b); sb("fr", C, _b); sb("fs", C, _b)
    sb("st", 54, _f); sb("sel", 54, _i); sb("xi", 54, _i); sb("xo", 54, _u)
    sb("n0", 54, _i); sb("n1", 54, _i); sb("dn", 54, _f); sb("bb", 54, _f); sb("b2", 54, _f)
    sb("fx", 3 * C, _b); sb("fxs", 3 * C, _b); sb("nt", 54, _f)
    sb("zn", 54, _i); sb("dz", 54, _f); sb("bz", 54, _f); sb("zf", 54, _f)
    sb("zt", 1536, _f); sb("mr", C, _f); sb("ms", C, _f); sb("mo", 18, _u)
    for r in range(4):
        sb("x%d" % r, 4 * C, _b)
    sb("qx", C, _q); sb("sx", C, _s); sb("qz", C, _q); sb("sz", C, _s)
    sb("xh", 4 * C, _b); sb("zp", 4 * C, _b); sb("z", 4 * C, _b); sb("h", 4 * C, _b); sb("d", 4 * C, _b)
    for r in range(3):
        sb("za%d" % r, 36, _u); sb("zb%d" % r, 18, _u); sb("la%d" % r, 36, _u); sb("lb%d" % r, 18, _u)
        sb("qh%d" % r, C, _q); sb("sh%d" % r, C, _s); sb("lq%d" % r, C, _q); sb("ls%d" % r, C, _s)
    sb("yt", C, _f); sb("owt", 3 * C, _f)
    d["ps"] = ("psum", [128, 4096], _f)
    return d


SCRATCH = _scratch()
_DMAS = ["x", "u", "v", "w", "wc", "ws", "y0", "y1", "ow", "oc", "os0", "os1", "os2", "os3"]
SEMAPHORES = (["qv", "qs", "qt", "qg", "loc"] + ["d" + n for n in _DMAS] +
              ["r%s%d" % (n, r) for n in ("a", "b", "q0", "q1", "s") for r in range(3)])


def rank_program(g, core, T, topo):
    rank = T.rank_of(core)
    if rank is None:
        return
    queue = {"v": g.vector, "s": g.scalar, "t": g.tensor, "g": g, "y": g.sync}
    count = {"v": 0, "s": 0, "t": 0, "g": 0}
    known = {q: {} for q in queue}
    snap, wrote, read, total, waited = {}, {}, {}, {}, {}

    def before(q, rd, wr):
        own = "q" + q
        deps = set(wrote[k] for k in rd if k in wrote)
        for k in wr:
            deps |= set(w for w in [wrote.get(k)] + read.get(k, []) if w and w[0] != own)
        best = {}
        for s, n in deps:
            if n > known[q].get(s, 0):
                best[s] = max(n, best.get(s, 0))
        for s, n in sorted(best.items()):
            if any(o != s and snap.get((o, m), {}).get(s, 0) >= n for o, m in best.items()):
                continue
            queue[q].wait_ge(T.sem[s], n)
            waited[s] = max(n, waited.get(s, 0))
            known[q][s] = n
            for o, m in snap.get((s, n), {}).items():
                known[q][o] = max(m, known[q].get(o, 0))

    def after(q, tag, rd, wr):
        snap[tag] = dict(known[q])
        total[tag[0]] = max(total.get(tag[0], 0), tag[1])
        for k in rd:
            read.setdefault(k, []).append(tag)
        for k in wr:
            wrote[k] = tag
            read[k] = []

    def op(q, fn, rd, wr):
        before(q, rd, wr)
        count[q] += 1
        fn(queue[q]).then_inc(T.sem["q" + q], 1)
        after(q, ("q" + q, count[q]), rd, wr)

    def dma(q, name, out, in_, rd, wr):
        before(q, rd, wr)
        queue[q].dma_start(out, in_).then_inc(T.sem["d" + name], 16)
        after(q, ("d" + name, 16), rd, wr)

    def tt(out, a, b, o, rd, wr):
        op("v", lambda e: e.tensor_tensor(out, a, b, o), rd, wr)

    def ts(out, a, s1, o1, rd, wr, s2=None, o2=None):
        if o2 is None:
            op("v", lambda e: e.tensor_scalar(out, a, s1, None, o1), rd, wr)
        else:
            op("v", lambda e: e.tensor_scalar(out, a, s1, s2, o1, o2), rd, wr)

    def cp(out, a, rd, wr):
        op("v", lambda e: e.tensor_copy(out, a), rd, wr)

    def fill(out, c, wr):
        op("v", lambda e: e.memset(out, c), [], wr)

    def ac(out, a, rd, wr, scale=1.0, bias=0.0, func=F.Copy):
        op("s", lambda e: e.activation(out, a, func, bias=bias, scale=scale), rd, wr)

    def scan(out, mask, v, rd, wr):
        op("v", lambda e: e.tensor_tensor_scan(out, mask, v, 0.0, A.add, A.max), rd, wr)

    def quant(q, s, x, rd, wr):
        op("v", lambda e: e.quantize_mx(q, s, x), rd, wr)

    def mm(bank, n, w, ws, x, xs, rd):
        op("t", lambda e: e.matmul_mx(T.ps[:, 512 * bank:512 * bank + n], w, ws, x, xs, True, True), rd, ["b%d" % bank])

    def bank(b, n=C):
        return T.ps[:, 512 * b:512 * b + n]

    def k18(k):
        return slice(18 * k, 18 * k + 18)

    def kc(k):
        return slice(C * k, C * k + C)

    dma("s", "w", T.wi[:], T.wl[:], [], ["wi"])
    dma("y", "x", T.x0[:], T.x[:], [], ["x0.%d" % b for b in range(4)])
    dma("s", "u", T.ut[:], T.u[:], [], ["ut"])
    dma("y", "wc", T.wq[:, 0:512].bitcast(dt.uint8), T.wc[:, 0:2048], [], ["wq"])
    dma("y", "ws", T.wsc[:, 0:512], T.ws[:, 0:512], [], ["wsc"])
    dma("y", "v", T.vt[:], T.v[:], [], ["vt"])

    def iota(out, pattern, base, cm, wr, small=False):
        if small:
            op("g", lambda e: e.iota(out, pattern, base, cm, allow_small_or_imprecise_dtypes=True), [], wr)
        else:
            op("g", lambda e: e.iota(out, pattern, base, cm), [], wr)
    iota(T.ei[:], [[1, 16]], 128, -1, ["ei"])
    iota(T.cr[:], [[1, C]], 0, 0, ["cr"], True)
    iota(T.i1[:], [[0, 18]], 0, 1, ["i1"])
    iota(T.i2[:], [[16, 18]], C, 0, ["i2"])
    iota(T.ui[:], [[1, 2], [16, 8]], 0, 0, ["ui"])
    iota(T.ones[:], [[0, 512]], 1, 0, ["ones"], True)
    for b in range(4):
        op("g", lambda e: e.affine_select(T.et[:, 512 * b:512 * b + 512], T.ones[:], [[-1, 512]], A.is_equal, 0.0, b, 4),
           ["ones"], ["et%d" % b])
    fill(T.t3[:, 0:C], 0.0, ["t3a"])
    fill(T.t3[:, C:2 * C], HUGE, ["t3b"])
    ts(T.ea[:], T.ei[:], 15, A.bitwise_and, ["ei"], ["ea"])
    ts(T.e0[:], T.ea[:], 0.0, A.is_equal, ["ea"], ["e0"], -4.0, A.mult)
    ts(T.e1[:], T.ea[:], 1.0, A.is_equal, ["ea"], ["e1"], 2.0, A.mult)
    ts(T.bp2[:, 0:1], T.ea[:, 15:16], 0.0, A.not_equal, ["ea"], ["bp2"], 2.0, A.mult)
    ts(T.bpn[:, 0:1], T.ea[:, 15:16], 0.0, A.not_equal, ["ea"], ["bpn"], 2.0 * BIG, A.mult)
    tt(T.mf[:, 0:16], T.e0[:], T.e1[:], A.add, ["e0", "e1"], ["mf"])
    for n in (16, 32, 64, 128, 256):
        m = min(n, C - n)
        cp(T.mf[:, n:n + m], T.mf[:, 0:m], ["mf"], ["mf"])
    for k in range(3):
        ts(T.mn[:, kc(k)], T.mf[:], BIG, A.mult, ["mf"], ["mn"])
    ts(T.i3[:], T.i1[:], 15, A.bitwise_and, ["i1"], ["i3"])
    cp(T.uo[:], T.ui[:], ["ui"], ["uo"])
    tt(T.cl[:], T.i3[:], T.i2[:], A.add, ["i3", "i2"], ["cl"])
    bp2, bpn = T.bp2[:, 0:1], T.bpn[:, 0:1]
    ac(T.t0[:, 0:C], T.cr[:], ["cr"], ["t0a"], 0.0, 512.0)
    ac(T.t0[:, C:], T.cr[:], ["cr"], ["t0b"], 0.0, 2048.0 * 512)
    ac(T.cr0[:], T.cr[:], ["cr"], ["cr0"], 2049.0)
    ac(T.t1[:, 0:C], T.cr[:], ["cr"], ["t1a"], 2048.0, 1024.0 + 2048 * 512)
    ac(T.t1[:, C:], T.cr[:], ["cr"], ["t1b"], 2048.0, 512.0)
    ac(T.t2[:, 0:C], T.cr[:], ["cr"], ["t2a"], 2048.0, 2048.0 * 1024)
    ac(T.t2[:, C:], T.cr[:], ["cr"], ["t2b"], 2048.0, 1024.0 + 2048 * 1024)
    for k in range(2):
        ac(T.pi[:, 512 * k + C:512 * k + 512], T.cr[:, 0:224], ["cr"], ["pig%d" % k])
    for k in range(2):
        ac(T.zt[:, 512 * k + C:512 * k + 512], T.cr[:, 0:224], ["cr"], ["ztg%d" % k])

    ts(T.c1[:], T.wi[:], float(C), A.is_ge, ["wi"], ["c1"], 224.0, A.mult)
    ts(T.c2[:], T.wi[:], 2.0 * C, A.is_ge, ["wi"], ["c2"], 224.0, A.mult)
    tt(T.c1[:], T.c1[:], T.wi[:], A.add, ["c1", "wi"], ["c3"])
    tt(T.new0[:], T.c1[:], T.c2[:], A.add, ["c3", "c2"], ["new0"])

    def lists(r):
        w0 = T["new%d" % (r % 2)][:, 0:18]
        w = "new%d" % (r % 2)
        tt(T.tl[:], w0, T.cl[:], A.subtract, [w, "cl"], ["tl"])
        ts(T.al[:], w0, 512.0, A.is_lt, [w], ["al"])
        tt(T.tm[:], T.tl[:], T.al[:], A.mult, ["tl", "al"], ["tm"])
        ts(T.qe[:, 0:18], T.al[:], 576.0, A.mult, ["al"], ["qe0"], -288.0, A.add)
        tt(T.dp[:], T.tm[:], T.cl[:], A.add, ["tm", "cl"], ["dp"])
        ts(T.qe[:, 18:36], T.al[:], 288.0, A.mult, ["al"], ["qe1"], 288.0, A.add)
        cp(T.do[:], T.dp[:], ["dp"], ["do"])

    def lists2():
        tt(T.ie[:, 0:18], T.qe[:, 0:18], T.dp[:], A.add, ["qe0", "dp"], ["ie0"])
        tt(T.ie[:, 18:36], T.qe[:, 18:36], T.dp[:], A.add, ["qe1", "dp"], ["ie1"])
        cp(T.ieo[:], T.ie[:], ["ie0", "ie1"], ["ieo"])

    def pis():
        for k in range(3):
            row = T.cr0 if k == 0 else T.cr
            t = T["t%d" % k]
            tt(T.pi[:, 512 * k:512 * k + C], t[:, 0:2 * C].indirect(T.do[:, 0:18]), row[:], A.add,
               ["do", "t%da" % k, "t%db" % k, "cr0" if k == 0 else "cr"], ["pi%d" % k])

    def thr():
        ac(T.thr[:], T.t3[:, 0:2 * C].indirect(T.do[:, 0:18]), ["do", "t3a", "t3b"], ["thr"])

    def nrow(r):
        o = "off%d" % (r % 2)
        rd = ["pi0", "pi1", "pi2", "pig0", "pig1", o]
        ac(T.nr[:, 0:2 * C], T.pi[:, 0:1024 + C].indirect(T[o][:, 0:36]), rd, ["nr0"])
        cp(T.nr[:, 2 * C:3 * C], T.pi[:, 0:1024 + C].indirect(T[o][:, 36:54]), rd, ["nr1"])

    def erow():
        ac(T.er[:], T.nr[:, 0:3 * C].indirect(T.ieo[:, 0:36]), ["nr0", "nr1", "ieo"], ["er"])

    def prep1():
        ns = T.ns
        scan(T.ns[:], T.mn[:], T.nr[:], ["mn", "nr0", "nr1"], ["ns"])
        tt(T.df[:, 18:54], ns[:, 15:576:16], ns[:, 303:864:16], A.subtract, ["ns"], ["df1"])
        tt(T.df[:, 0:18], ns[:, 591:864:16], ns[:, 15:288:16], A.subtract, ["ns"], ["df0"])
        for k in (1, 2, 0):
            tt(T.dg[:, k18(k)], T.df[:, k18(k)], T.al[:], A.mult, ["df0" if k == 0 else "df1", "al"], ["dg%d" % k])

    def base():
        tt(T.base[:], T.dg[:], T.ns[:, 15:864:16], A.add, ["dg0", "dg1", "dg2", "ns"], ["base"])

    def halves(r):
        for b in range(4):
            ac(T.xh[:, kc(b)], T["x%d" % r][:, b:4 * C:4], ["x%d.%d" % (r, b)], ["xh%d" % b], 0.5)

    def qstate(r):
        quant(T.qx[:, 0:C], T.sx[:, 0:C], T["x%d" % r][:, 0:4 * C], ["x%d.%d" % (r, b) for b in range(4)], ["qx"])

    def scores():
        for k in (1, 0):
            mm(k, C, T.u2[:, 128 * k:128 * k + 128], T.u2s[:, 128 * k:128 * k + 128], T.qx[:, 0:C], T.sx[:, 0:C],
               ["u2", "u2s", "qx"])

    lists(0)
    cp(T.off0[:], T.new0[:], ["new0"], ["off0"])
    lists2()
    thr()
    quant(T.uq[:, 0:128], T.us[:, 0:128], T.ut[:, 0:512], ["ut"], ["uq"])
    op("s", lambda e: e.activation(T.u2s[:, 0:256], T.us[:, 0:128].indirect(T.uo[:, 0:16]), F.Copy), ["uq", "uo"], ["u2s"])
    pis()
    nrow(0)
    op("v", lambda e: e.tensor_copy(T.u2[:, 0:256].bitcast(dt.uint32), T.uq[:, 0:128].bitcast(dt.uint32).indirect(T.uo[:, 0:16])),
       ["uq", "uo"], ["u2"])
    qstate(0)
    scores()
    erow()
    prep1()
    base()

    for r in range(3):
        peer = T.cores[rank ^ STEP[r]]
        rid, pid = topo.addr(peer, core)
        mask = topo.mask(core, peer)
        arrive = len(topo.engines(peer, core))
        last = r == 2

        def send(dst, src, sem, rd):
            before("g", rd, [])
            g.remote_dma(out_ap=dst, in_ap=src, remote_sem=T.sem[sem], local_sem=T.sem.loc, pid=pid, routing_id=rid,
                         dma_engine_mask=mask)
            total["loc"] = total.get("loc", 0) + len(topo.engines(core, peer))

        def arrival(sem, key):
            wrote[key] = (sem, arrive)
            snap[(sem, arrive)] = {}
            total[sem] = arrive
        arrival("ra%d" % r, "la")
        arrival("rb%d" % r, "lb")
        for i in range(2):
            arrival("rq%d%d" % (i, r), "lq%d" % i)
        arrival("rs%d" % r, "ls")
        n = (r + 1) % 2
        new, off, za, zb = T["new%d" % n], T["off%d" % n], T["za%d" % r], T["zb%d" % r]
        lq, ls, qh, sh = T["lq%d" % r], T["ls%d" % r], T["qh%d" % r], T["sh%d" % r]

        ac(T.a2[:, C:2 * C], bank(1), ["b1"], ["a2b"], func=F.Relu)
        halves(r)
        scan(T.es[:], T.mn[:, 0:2 * C], T.er[:], ["mn", "er"], ["es"])
        tt(T.am[:], bank(0), T.thr[:], A.is_gt, ["b0", "thr"], ["am"])
        tt(T.dl[:, 18:54], T.es[:, 15:576:16], T.base[:, 18:54], A.subtract, ["es", "base"], ["dl1"])
        tt(T.dl[:, 0:18], T.base[:, 18:36], T.base[:, 0:18], A.subtract, ["base"], ["dl0"])
        cp(T.a2[:, 0:C], T.am[:], ["am"], ["a2a"])
        ts(T.bd[:], T.dl[:], bp2, A.mult, ["dl0", "dl1", "bp2", "bpn"], ["bd"], bpn, A.add)
        tt(T.base2[:], T.base[:], T.bd[:], A.subtract, ["base", "bd"], ["base2"])
        tt(T.fr[:], T.a2[:, 0:2 * C].indirect(T.do[:, 0:18]), T.am[:], A.not_equal, ["a2a", "a2b", "am", "do"], ["fr"])
        scan(T.fs[:], T.mf[:], T.fr[:], ["mf", "fr"], ["fs"])

        for k in (1, 2, 0):
            tt(T.st[:, k18(k)], T.fs[:, 15:C:16], T.dl[:, k18(k)], A.mult, ["fs", "dl0", "dl1"], ["st%d" % k])
        tt(T.sel[:], T.st[:], T.base2[:], A.add, ["st0", "st1", "st2", "base2"], ["sel"])
        ts(T.xi[:], T.sel[:], 511, A.bitwise_and, ["sel"], ["xi"])
        cp(T.xo[:], T.xi[:], ["xi"], ["xo"])
        for k in (1, 2, 0):
            ac(T.fx[:, kc(k)], T.fr[:, 0:C].indirect(T.xo[:, k18(k)]), ["fr", "xo"], ["fx%d" % k])
        ts(T.zn[:], T.sel[:], 11, A.logical_shift_right, ["sel"], ["zn"], 511, A.bitwise_and)
        tt(T.dz[:], T.zn[:], T.xi[:], A.subtract, ["zn", "xi"], ["dz"])
        ts(T.bb[:], T.dz[:], bp2, A.mult, ["dz", "bp2"], ["bb"])
        tt(T.bz[:], T.xi[:], T.bb[:], A.subtract, ["xi", "bb"], ["bz"])

        def fscan(k):
            scan(T.fxs[:, kc(k)], T.mf[:], T.fx[:, kc(k)], ["mf", "fx%d" % k], ["fxs%d" % k])

        def zmul(k):
            tt(T.zf[:, k18(k)], T.fxs[:, C * k + 15:C * k + C:16], T.dz[:, k18(k)], A.mult, ["fxs%d" % k, "dz"], ["zm%d" % k])

        def zadd(k):
            tt(T.zf[:, k18(k)], T.zf[:, k18(k)], T.bz[:, k18(k)], A.add, ["zm%d" % k, "bz"], ["zf%d" % k])

        def zout(k):
            cp(zb[:] if k == 0 else za[:, k18(k - 1)], T.zf[:, k18(k)], ["zf%d" % k], ["zo%d" % k])
        fscan(1)
        zmul(1)
        fscan(2)
        zadd(1)
        zmul(2)
        zout(1)
        zadd(2)
        zout(2)
        send(T["la%d" % r][:], za[:], "ra%d" % r, ["zo1", "zo2"])

        def hquant(i):
            a, e = CUT[i]
            quant(qh[:, a:e], sh[:, a:e], T.h[:, 4 * a:4 * e], ["h%d%d" % (i, b) for b in range(4)], ["qh%d" % i])
            send(lq[:, a:e].bitcast(dt.uint8), qh[:, a:e].bitcast(dt.uint8), "rq%d%d" % (i, r), ["qh%d" % i])
            if i == 1:
                send(ls[:, 0:C], sh[:, 0:C], "rs%d" % r, ["qh0", "qh1"])
        for i, (a, e) in enumerate(CUT):
            for b in range(4):
                ac(T.zp[:, C * b + a:C * b + e], T.xh[:, kc(b)].indirect(za[:, a // 16:e // 16]),
                   ["xh%d" % b, "zo1"], ["zp%d%d" % (i, b)])
                tt(T.z[:, 4 * a + b:4 * e:4], T.xh[:, kc(b)].indirect(za[:, 18 + a // 16:18 + e // 16]),
                   T.zp[:, C * b + a:C * b + e], A.add, ["xh%d" % b, "zo2", "zp%d%d" % (i, b)], ["z%d" % i])
            quant(T.qz[:, a:e], T.sz[:, a:e], T.z[:, 4 * a:4 * e], ["z%d" % i], ["qz%d" % i])
        for i, (a, e) in enumerate(CUT):
            for b in range(4):
                k = (2 + 4 * i + b) % 8
                mm(k, e - a, T.wq[:, 128 * b:128 * b + 128], T.wsc[:, 128 * b:128 * b + 128], T.qz[:, a:e], T.sz[:, a:e],
                   ["wq", "wsc", "qz%d" % i])
                ac(T.h[:, 4 * a + b:4 * e:4], bank(k, e - a), ["b%d" % k], ["h%d%d" % (i, b)], 0.03125)
        fscan(0)
        ts(T.n0[:], T.sel[:], 2047, A.bitwise_and, ["sel"], ["n0"])
        ts(T.n1[:], T.sel[:], 11, A.logical_shift_right, ["sel"], ["n1"])
        zmul(0)
        tt(T.dn[:], T.n1[:], T.n0[:], A.subtract, ["n1", "n0"], ["dn"])
        hquant(0)
        zadd(0)
        ts(T.bb[:], T.dn[:], bp2, A.mult, ["dn", "bp2"], ["bb"])
        tt(T.nt[:], T.fxs[:, 15:3 * C:16], T.dn[:], A.mult, ["fxs0", "fxs1", "fxs2", "dn"], ["nt"])
        zout(0)
        send(T["lb%d" % r][:], zb[:], "rb%d" % r, ["zo0"])
        tt(T.b2[:], T.n0[:], T.bb[:], A.subtract, ["n0", "bb"], ["b2"])
        hquant(1)
        tt(new[:], T.nt[:], T.b2[:], A.add, ["nt", "b2"], ["new%d" % n])
        cp(off[:], new[:], ["new%d" % n], ["off%d" % n])

        if r == 0:
            iota(T.pt[:], [[C, 3], [1, 512]], 0, 0, ["pt"], True)
        if not last:
            lists(r + 1)
            pis()
            lists2()
            thr()
        for k in (1, 2):
            ac(T.zt[:, 512 * k:512 * k + C], T.cr[:, 0:C].indirect(T["la%d" % r][:, k18(k - 1)]), ["cr", "la"], ["zt%d" % k])
        if r == 0:
            quant(T.eq[:, 0:512], T.esc[:, 0:512], T.et[:, 0:2048], ["et%d" % b for b in range(4)], ["eq"])
        if last:
            quant(T.vq[:, 0:128], T.vs[:, 0:128], T.vt[:, 0:512], ["vt"], ["vq"])
        if not last:
            nrow(r + 1)
        ac(T.zt[:, 0:C], T.cr[:, 0:C].indirect(T["lb%d" % r][:, 0:18]), ["cr", "lb"], ["zt0"])
        ac(T.mr[:], T.zt[:, 0:1024 + C].indirect(off[:, 0:18]), ["zt0", "zt1", "zt2", "ztg0", "ztg1", "off%d" % n], ["mr"])
        if not last:
            prep1()
        scan(T.ms[:], T.mn[:, 0:C], T.mr[:], ["mn", "mr"], ["ms"])
        if not last:
            base()
        ts(T.mo[:], T.ms[:, 15:C:16], bpn, A.subtract, ["ms", "bpn"], ["mo"])
        if last:
            ac(T.owt[:], T.pt[:, 0:1024 + C].indirect(off[:, 0:54]), ["pt", "off%d" % n], ["owt"])
            dma("y", "ow", T.ow[:], T.owt[0:128:16, :], ["owt"], [])

        x, y = "x%d" % r, "x%d" % (r + 1)
        for b in range(4):
            k = 2 + b
            mm(k, C, T.eq[:, 128 * b:128 * b + 128], T.esc[:, 128 * b:128 * b + 128], lq[:, 0:C], ls[:, 0:C],
               ["eq", "lq0", "lq1", "ls"])
            ac(T.d[:, kc(b)], bank(k), ["b%d" % k], ["d%d" % b])
        if not last:
            erow()
        for b in range(4):
            tt(T[y][:, b:4 * C:4], T.d[:, kc(b)].indirect(T.mo[:, 0:18]), T[x][:, b:4 * C:4], A.add,
               ["d%d" % b, "mo", "%s.%d" % (x, b)], ["%s.%d" % (y, b)])
        qstate(r + 1)
        if not last:
            scores()

    h = C // 2
    for i in range(2):
        mm(2 + i, h, T.vq[:, 0:128], T.vs[:, 0:128], T.qx[:, h * i:h * i + h], T.sx[:, h * i:h * i + h], ["vq", "qx"])
    dma("y", "oc", T.oc[:, 0:4 * C], T.qx[:, 0:C].bitcast(dt.uint8), ["qx"], [])
    for k in range(4):
        dma("y", "os%d" % k, T.osc[4 * k:4 * k + 4, 0:C], T.sx[32 * k:32 * k + 4, 0:C], ["qx"], [])
    cp(T.yt[:, h:C], bank(3, h), ["b3"], ["yt1"])
    ac(T.yt[:, 0:h], bank(2, h), ["b2"], ["yt0"])
    dma("s", "y0", T.y[:, 0:h], T.yt[:, 0:h], ["yt0"], [])
    dma("s", "y1", T.y[:, h:C], T.yt[:, h:C], ["yt1"], [])
    for s, m in sorted(total.items()):
        if waited.get(s, 0) < m:
            g.wait_ge(T.sem[s], m)
